import numpy as np
import ml_dtypes


def mxq(x, axis, fmt="e4m3"):
    dtype, down = {"e4m3": (ml_dtypes.float8_e4m3fn, 7), "e5m2": (ml_dtypes.float8_e5m2, 14)}[fmt]
    v = np.moveaxis(np.asarray(x, np.float32).astype(ml_dtypes.bfloat16).astype(np.float64), axis, -1)
    blocks = v.reshape(v.shape[:-1] + (-1, 32))
    amax = np.abs(blocks).max(-1, keepdims=True)
    byte = np.maximum(np.where(amax > 0, np.frexp(amax)[1] - 1 + 127, 0) - down, 1)
    scale = np.exp2(byte - 127.0)
    codes = (blocks / scale).astype(np.float32).astype(dtype).astype(np.float64)
    return np.moveaxis((codes * scale).reshape(v.shape), -1, axis)


WIDE = False


def mx_kscale(k):
    if not WIDE:
        return np.ones(k)
    levels = np.array([10, -10, 5, -5, 0])
    if k % 512:
        return np.exp2(np.random.permutation(np.resize(levels, k // 32))).repeat(32)
    a = np.empty((k // 512, 16))
    for p in range(k // 512):
        a[p, :8] = np.random.permutation(np.resize(levels, 8))
        for g in range(8):
            far = levels[np.abs(levels - a[p, g]) >= 10]
            a[p, g + 8] = far[np.random.randint(len(far))]
    return np.exp2(a.ravel()).repeat(32)


def f64(x):
    return np.asarray(x).astype(np.float64)


def striped(idx):
    return np.tile(np.asarray(idx).reshape(-1, 16).T, (8, 1)).astype(np.uint16)


def unstriped(offs):
    return offs[:16].T.reshape(-1).astype(np.int64)


E2M1 = np.array([0.0, 0.5, 1.0, 1.5, 2.0, 3.0, 4.0, 6.0, -0.0, -0.5, -1.0, -1.5, -2.0, -3.0, -4.0, -6.0])


def pack_weight(w, fmt):
    k, n = w.shape
    w = f64(np.asarray(w, np.float32).astype(ml_dtypes.bfloat16)).reshape(k // 32, 32, n)
    amax = np.abs(w).max(1)
    if fmt == "e4m3":
        byte = np.frexp(amax)[1] - 1 + 127 - 7
    else:
        mant, ex = np.frexp(amax / 6.0)
        byte = np.where(mant > 0.5, ex, ex - 1) + 127
    byte = np.clip(np.where(amax > 0, byte, 1), 1, 254)
    scaled = (w * np.exp2(127.0 - byte)[:, None, :]).reshape(k, n).astype(np.float32)
    by_word = np.ascontiguousarray(scaled.reshape(k // 512, 128, 4, n).transpose(0, 1, 3, 2))
    if fmt == "e4m3":
        words = by_word.astype(ml_dtypes.float8_e4m3fn).view(np.uint8)
    else:
        c = by_word.astype(ml_dtypes.float4_e2m1fn).view(np.uint8) & 0xF
        words = (c[..., 0::2] | (c[..., 1::2] << 4)).reshape(k // 512, 128, 2 * n)
    return np.ascontiguousarray(words), np.ascontiguousarray(byte.astype(np.uint8).reshape(k // 512, 16, n))


def unpack_weight(words, scales, fmt):
    g, _, n = scales.shape
    words = np.ascontiguousarray(words).reshape(g, 128, n, -1)
    if fmt == "e4m3":
        vals = words.view(ml_dtypes.float8_e4m3fn).astype(np.float64)
    else:
        nib = np.empty((g, 128, n, 4), np.uint8)
        nib[..., 0::2] = words & 0xF
        nib[..., 1::2] = words >> 4
        vals = E2M1[nib]
    vals = vals * np.repeat(np.exp2(scales.astype(np.float64) - 127.0), 8, axis=1)[..., None]
    return vals.transpose(0, 1, 3, 2).reshape(g * 512, n)


D, T, I, Q = 512, 2048, 512, 128


def setup_inputs():
    n = np.random.standard_normal
    idx = np.random.permutation(T)[:I]
    fd = mx_kscale(D)
    keysp = pack_weight(n((D, T)) / fd[:, None], "e2m1")
    return {
        "query": (n((D, Q)) * 0.8 / np.sqrt(D) * fd[:, None]).astype(np.float32),
        "keys_words": keysp[0],
        "keys_scales": keysp[1],
        "mass": (np.random.uniform(0.0, 2.0, (Q, T))).astype(np.float32),
        "dec": (np.random.uniform(0.8, 1.0, (Q, 1))).astype(np.float32),
        "offs": striped(idx),
    }


def reference(query, keys_words, keys_scales, mass, dec, offs):
    idx = unstriped(offs)
    keysu = unpack_weight(keys_words, keys_scales, "e2m1")
    queryq = mxq(f64(query), 0, "e4m3")
    keysidxg = keysu[:, idx]
    a = queryq.T @ keysidxg
    p = np.exp(a - np.max(a, axis=1, keepdims=True))
    w = p / np.sum(p, axis=1, keepdims=True) * 512.0
    wf = np.zeros((Q, T))
    wf[:, idx] = w
    y = f64(dec) * f64(mass) + wf
    return y

@@ -1,0 +1,126 @@
+from contextlib import ExitStack
+
+import concourse.mybir as mybir
+
+D, T, I, Q = 512, 2048, 512, 128
+FLOPS = 2 * D * I * Q
+
+F32 = mybir.dt.float32
+BF16 = mybir.dt.bfloat16
+I32 = mybir.dt.int32
+U32 = mybir.dt.uint32
+U16 = mybir.dt.uint16
+U8 = mybir.dt.uint8
+FP8X4 = mybir.dt.float8_e4m3fn_x4
+FP4X4 = mybir.dt.float4_e2m1fn_x4
+ALU = mybir.AluOpType
+ACT = mybir.ActivationFunctionType
+
+P = 128
+PACK = 4
+HALF = I // 2
+OUT_WIDTHS = (256, 512, 512, 512, 256)
+
+
+def tile_attend_heavyhitter_kernel(tc, query, keys_words, keys_scales, mass, dec, offs, out):
+    nc = tc.nc
+    with ExitStack() as ctx:
+        sb = ctx.enter_context(tc.tile_pool(name="sb", bufs=1))
+        ps = ctx.enter_context(tc.psum_pool(name="ps", bufs=1))
+
+        offsets = sb.tile([P, I // 16], U16, name="offsets")
+        pool_words = sb.tile([P, T], U16, name="pool_words", align_bytes=64)
+        pool_scales = sb.tile([P, T], U8, name="pool_scales", align_bytes=64)
+        q_raw = sb.tile([P, PACK, Q], F32, name="q_raw", tag="raw")
+        decay = sb.tile([P, 1], F32, name="decay")
+        window = sb.tile([P, T], F32, name="window")
+
+        nc.vector.memset(pool_scales[:].bitcast(I32), 0)
+        nc.sync.dma_start(out=pool_words[:].bitcast(I32), in_=keys_words[0].bitcast(I32))
+        nc.sync.dma_start(offsets[:], offs)
+        nc.sync.dma_start(out=q_raw[:], in_=query.rearrange("(p j) h -> p j h", j=PACK))
+        for r in range(4):
+            nc.sync.dma_start(out=pool_scales[r:P:32, :].bitcast(I32), in_=keys_scales[0, r:16:4, :].bitcast(I32))
+        nc.scalar.dma_start(out=decay[:], in_=dec)
+        nc.vector.memset(window[:], 0.0)
+
+        q_grouped = sb.tile([P, Q, PACK], BF16, name="q_grouped", align_bytes=64)
+        nc.scalar.activation(
+            q_grouped[:].rearrange("p (c i) t -> p c t i", i=4),
+            q_raw[:].rearrange("p t (c i) -> p c t i", i=4),
+            ACT.Copy,
+        )
+        old = sb.tile([P, T], F32, name="old", tag="raw")
+        for c in range(2):
+            cols = slice(c * (T // 2), (c + 1) * (T // 2))
+            nc.sync.dma_start(out=old[:, cols], in_=mass[:, cols])
+
+        k_words = sb.tile([P, I], U16, name="k_words", align_bytes=64)
+        nc.vector.tensor_copy(k_words[:], pool_words[:].indirect(offsets[:]))
+        q_codes = sb.tile([P, Q], U32, name="q_codes", align_bytes=64)
+        q_scales = sb.tile([P, Q], U8, name="q_scales", align_bytes=64)
+
+        lists = [offsets[:, h * (HALF // 16) : (h + 1) * (HALF // 16)] for h in range(2)]
+        banks = []
+        for h in range(2):
+            k_scales = sb.tile([P, HALF], U8, name="k_scales%d" % h, align_bytes=64)
+            nc.vector.tensor_copy(k_scales[:], pool_scales[:].indirect(lists[h]))
+            if h == 0:
+                nc.vector.quantize_mx(
+                    out=q_codes[:].bitcast(FP8X4), scales=q_scales[:], in_=q_grouped[:].rearrange("p h t -> p (h t)")
+                )
+            bank = ps.tile([P, HALF], F32, name="bank%d" % h)
+            nc.tensor.matmul_mx(
+                out=bank[:],
+                lhsT=q_codes[:].bitcast(FP8X4),
+                lhsT_scale=q_scales[:],
+                rhs=k_words[:, h * HALF : (h + 1) * HALF].bitcast(FP4X4),
+                rhs_scale=k_scales[:],
+                start=True,
+                stop=True,
+            )
+            banks.append(bank)
+
+        neg_max0 = sb.tile([P, 1], F32, name="neg_max0")
+        neg_max = sb.tile([P, 1], F32, name="neg_max")
+        neg_scores1 = sb.tile([P, HALF], F32, name="neg_scores1")
+        nc.vector.tensor_reduce(out=neg_max0[:], in_=banks[0][:], axis=mybir.AxisListType.X, op=ALU.max, negate=True)
+        nc.vector.tensor_scalar(
+            out=neg_scores1[:], in0=banks[1][:], scalar1=-1.0, scalar2=neg_max0[:], op0=ALU.mult, op1=ALU.min,
+            accum_out=neg_max[:],
+        )
+
+        sums = []
+        for h, (src, sign) in enumerate(((banks[0], 1.0), (neg_scores1, -1.0))):
+            p = sb.tile([P, HALF], F32, name="p%d" % h)
+            s = sb.tile([P, 1], F32, name="sum%d" % h)
+            nc.scalar.activation(p[:], src[:], ACT.Exp, bias=neg_max[:], scale=sign, accum_out=s[:])
+            nc.vector.tensor_copy(window[:].indirect(lists[h]), p[:])
+            sums.append(s)
+        total = sb.tile([P, 1], F32, name="total")
+        gain = sb.tile([P, 1], F32, name="gain")
+        nc.vector.tensor_scalar(
+            out=total[:], in0=sums[0][:], scalar1=sums[1][:], scalar2=1.0 / I, op0=ALU.add, op1=ALU.mult
+        )
+        nc.vector.reciprocal(gain[:], total[:])
+
+        decayed = []
+        for c in range(2):
+            part = sb.tile([P, T // 2], F32, name="decayed%d" % c)
+            nc.scalar.activation(part[:], old[:, c * (T // 2) : (c + 1) * (T // 2)], ACT.Copy, scale=decay[:])
+            decayed.append(part)
+
+        lo = 0
+        for n, width in enumerate(OUT_WIDTHS):
+            res = sb.tile([P, width], F32, name="res%d" % n)
+            done = 0
+            while done < width:
+                c, at = divmod(lo + done, T // 2)
+                take = min(width - done, T // 2 - at)
+                nc.vector.scalar_tensor_tensor(
+                    out=res[:, done : done + take], in0=window[:, lo + done : lo + done + take], scalar=gain[:],
+                    in1=decayed[c][:, at : at + take], op0=ALU.mult, op1=ALU.add,
+                )
+                done = done + take
+            nc.sync.dma_start(out=out[:, lo : lo + width], in_=res[:])
+            lo = lo + width

@@ -19,7 +19,8 @@ ACT = mybir.ActivationFunctionType
 P = 128
 PACK = 4
 HALF = I // 2
-OUT_WIDTHS = (256, 512, 512, 512, 256)
+HEADROOM = 32.0
+OUT_WIDTHS = (128, 384, 512, 512, 384, 128)
 
 
 def tile_attend_heavyhitter_kernel(tc, query, keys_words, keys_scales, mass, dec, offs, out):
@@ -49,6 +50,7 @@ def tile_attend_heavyhitter_kernel(tc, query, keys_words, keys_scales, mass, dec
             q_grouped[:].rearrange("p (c i) t -> p c t i", i=4),
             q_raw[:].rearrange("p t (c i) -> p c t i", i=4),
             ACT.Copy,
+            scale=-1.0,
         )
         old = sb.tile([P, T], F32, name="old", tag="raw")
         for c in range(2):
@@ -81,28 +83,29 @@ def tile_attend_heavyhitter_kernel(tc, query, keys_words, keys_scales, mass, dec
             )
             banks.append(bank)
 
-        neg_max0 = sb.tile([P, 1], F32, name="neg_max0")
-        neg_max = sb.tile([P, 1], F32, name="neg_max")
-        neg_scores1 = sb.tile([P, HALF], F32, name="neg_scores1")
-        nc.vector.tensor_reduce(out=neg_max0[:], in_=banks[0][:], axis=mybir.AxisListType.X, op=ALU.max, negate=True)
-        nc.vector.tensor_scalar(
-            out=neg_scores1[:], in0=banks[1][:], scalar1=-1.0, scalar2=neg_max0[:], op0=ALU.mult, op1=ALU.min,
-            accum_out=neg_max[:],
-        )
+        bias = []
+        for h in range(2):
+            spare = sb.tile([P, HALF], F32, name="spare%d" % h)
+            low = sb.tile([P, 1], F32, name="bias%d" % h)
+            nc.vector.tensor_scalar(
+                out=spare[:], in0=banks[h][:], scalar1=(-HEADROOM, 0.0)[h], scalar2=bias[0][:] if h else None,
+                op0=ALU.add, op1=ALU.min, accum_out=low[:],
+            )
+            bias.append(low)
 
         sums = []
-        for h, (src, sign) in enumerate(((banks[0], 1.0), (neg_scores1, -1.0))):
+        for h in range(2):
             p = sb.tile([P, HALF], F32, name="p%d" % h)
             s = sb.tile([P, 1], F32, name="sum%d" % h)
-            nc.scalar.activation(p[:], src[:], ACT.Exp, bias=neg_max[:], scale=sign, accum_out=s[:])
+            nc.scalar.activation(p[:], banks[h][:], ACT.Exp, bias=bias[h][:], scale=-1.0, accum_out=s[:])
             nc.vector.tensor_copy(window[:].indirect(lists[h]), p[:])
             sums.append(s)
         total = sb.tile([P, 1], F32, name="total")
+        mean = sb.tile([P, 1], F32, name="mean")
         gain = sb.tile([P, 1], F32, name="gain")
-        nc.vector.tensor_scalar(
-            out=total[:], in0=sums[0][:], scalar1=sums[1][:], scalar2=1.0 / I, op0=ALU.add, op1=ALU.mult
-        )
-        nc.vector.reciprocal(gain[:], total[:])
+        nc.scalar.activation(total[:], sums[0][:], ACT.Identity, bias=sums[1][:])
+        nc.scalar.activation(mean[:], total[:], ACT.Copy, scale=1.0 / I)
+        nc.vector.reciprocal(gain[:], mean[:])
 
         decayed = []
         for c in range(2):

@@ -20,7 +20,7 @@ P = 128
 PACK = 4
 HALF = I // 2
 HEADROOM = 32.0
-OUT_WIDTHS = (128, 384, 512, 512, 384, 128)
+OUT_WIDTHS = (128, 256, 256, 384, 512, 512)
 
 
 def tile_attend_heavyhitter_kernel(tc, query, keys_words, keys_scales, mass, dec, offs, out):
@@ -33,7 +33,6 @@ def tile_attend_heavyhitter_kernel(tc, query, keys_words, keys_scales, mass, dec
         pool_words = sb.tile([P, T], U16, name="pool_words", align_bytes=64)
         pool_scales = sb.tile([P, T], U8, name="pool_scales", align_bytes=64)
         q_raw = sb.tile([P, PACK, Q], F32, name="q_raw", tag="raw")
-        decay = sb.tile([P, 1], F32, name="decay")
         window = sb.tile([P, T], F32, name="window")
 
         nc.vector.memset(pool_scales[:].bitcast(I32), 0)
@@ -42,7 +41,6 @@ def tile_attend_heavyhitter_kernel(tc, query, keys_words, keys_scales, mass, dec
         nc.sync.dma_start(out=q_raw[:], in_=query.rearrange("(p j) h -> p j h", j=PACK))
         for r in range(4):
             nc.sync.dma_start(out=pool_scales[r:P:32, :].bitcast(I32), in_=keys_scales[0, r:16:4, :].bitcast(I32))
-        nc.scalar.dma_start(out=decay[:], in_=dec)
         nc.vector.memset(window[:], 0.0)
 
         q_grouped = sb.tile([P, Q, PACK], BF16, name="q_grouped", align_bytes=64)
@@ -52,7 +50,9 @@ def tile_attend_heavyhitter_kernel(tc, query, keys_words, keys_scales, mass, dec
             ACT.Copy,
             scale=-1.0,
         )
-        old = sb.tile([P, T], F32, name="old", tag="raw")
+        old = sb.tile([P, T + 8], F32, name="old", tag="raw")
+        decay = old[:, T : T + 1]
+        nc.sync.dma_start(out=decay, in_=dec)
         for c in range(2):
             cols = slice(c * (T // 2), (c + 1) * (T // 2))
             nc.sync.dma_start(out=old[:, cols], in_=mass[:, cols])
@@ -110,7 +110,7 @@ def tile_attend_heavyhitter_kernel(tc, query, keys_words, keys_scales, mass, dec
         decayed = []
         for c in range(2):
             part = sb.tile([P, T // 2], F32, name="decayed%d" % c)
-            nc.scalar.activation(part[:], old[:, c * (T // 2) : (c + 1) * (T // 2)], ACT.Copy, scale=decay[:])
+            nc.scalar.activation(part[:], old[:, c * (T // 2) : (c + 1) * (T // 2)], ACT.Copy, scale=decay)
             decayed.append(part)
 
         lo = 0

@@ -19,6 +19,7 @@ ACT = mybir.ActivationFunctionType
 P = 128
 PACK = 4
 HALF = I // 2
+LEAD = 128
 HEADROOM = 32.0
 OUT_WIDTHS = (128, 256, 256, 384, 512, 512)
 
@@ -42,6 +43,8 @@ def tile_attend_heavyhitter_kernel(tc, query, keys_words, keys_scales, mass, dec
         for r in range(4):
             nc.sync.dma_start(out=pool_scales[r:P:32, :].bitcast(I32), in_=keys_scales[0, r:16:4, :].bitcast(I32))
         nc.vector.memset(window[:], 0.0)
+        zeros = sb.tile([P, LEAD], F32, name="zeros")
+        nc.vector.memset(zeros[:], 0.0)
 
         q_grouped = sb.tile([P, Q, PACK], BF16, name="q_grouped", align_bytes=64)
         nc.scalar.activation(
@@ -83,28 +86,29 @@ def tile_attend_heavyhitter_kernel(tc, query, keys_words, keys_scales, mass, dec
             )
             banks.append(bank)
 
-        bias = []
-        for h in range(2):
-            spare = sb.tile([P, HALF], F32, name="spare%d" % h)
-            low = sb.tile([P, 1], F32, name="bias%d" % h)
-            nc.vector.tensor_scalar(
-                out=spare[:], in0=banks[h][:], scalar1=(-HEADROOM, 0.0)[h], scalar2=bias[0][:] if h else None,
-                op0=ALU.add, op1=ALU.min, accum_out=low[:],
-            )
-            bias.append(low)
-
-        sums = []
-        for h in range(2):
-            p = sb.tile([P, HALF], F32, name="p%d" % h)
-            s = sb.tile([P, 1], F32, name="sum%d" % h)
-            nc.scalar.activation(p[:], banks[h][:], ACT.Exp, bias=bias[h][:], scale=-1.0, accum_out=s[:])
-            nc.vector.tensor_copy(window[:].indirect(lists[h]), p[:])
-            sums.append(s)
-        total = sb.tile([P, 1], F32, name="total")
+        first = sb.tile([P, 1], F32, name="first")
+        nc.vector.tensor_reduce(out=first[:], in_=banks[0][:], axis=mybir.AxisListType.X, op=ALU.min)
+        spare = sb.tile([P, HALF], F32, name="spare")
+        second = sb.tile([P, 1], F32, name="second")
+        nc.vector.tensor_scalar(
+            out=spare[:], in0=banks[1][:], scalar1=HEADROOM, scalar2=first[:], op0=ALU.add, op1=ALU.min,
+            accum_out=second[:],
+        )
+        terms = sb.tile([P, I], F32, name="terms")
+        sums = sb.tile([P, 3], F32, name="sums")
+        nc.scalar.activation(
+            terms[:, :LEAD], banks[0][:, :LEAD], ACT.Exp, bias=first[:], scale=-1.0, accum_out=sums[:, 0:1]
+        )
+        nc.vector.tensor_tensor(window[:].indirect(offsets[:, : LEAD // 16]), terms[:, :LEAD], zeros[:], ALU.add)
+        nc.scalar.activation(
+            terms[:, LEAD:HALF], banks[0][:, LEAD:], ACT.Exp, bias=first[:], scale=-1.0, accum_out=sums[:, 1:2]
+        )
+        nc.scalar.activation(terms[:, HALF:], banks[1][:], ACT.Exp, bias=second[:], scale=-1.0, accum_out=sums[:, 2:3])
+        nc.vector.tensor_copy(window[:].indirect(offsets[:, LEAD // 16 :]), terms[:, LEAD:])
+        shares = sb.tile([P, 3], F32, name="shares")
         mean = sb.tile([P, 1], F32, name="mean")
         gain = sb.tile([P, 1], F32, name="gain")
-        nc.scalar.activation(total[:], sums[0][:], ACT.Identity, bias=sums[1][:])
-        nc.scalar.activation(mean[:], total[:], ACT.Copy, scale=1.0 / I)
+        nc.scalar.activation(shares[:], sums[:], ACT.Copy, scale=1.0 / I, accum_out=mean[:])
         nc.vector.reciprocal(gain[:], mean[:])
 
         decayed = []

@@ -46,6 +46,9 @@ def tile_attend_heavyhitter_kernel(tc, query, keys_words, keys_scales, mass, dec
         zeros = sb.tile([P, LEAD], F32, name="zeros")
         nc.vector.memset(zeros[:], 0.0)
 
+        minus_one = sb.tile([P, 1], F32, name="minus_one")
+        nc.gpsimd.memset(minus_one[:], -1.0)
+
         q_grouped = sb.tile([P, Q, PACK], BF16, name="q_grouped", align_bytes=64)
         nc.scalar.activation(
             q_grouped[:].rearrange("p (c i) t -> p c t i", i=4),
@@ -109,7 +112,7 @@ def tile_attend_heavyhitter_kernel(tc, query, keys_words, keys_scales, mass, dec
         mean = sb.tile([P, 1], F32, name="mean")
         gain = sb.tile([P, 1], F32, name="gain")
         nc.scalar.activation(shares[:], sums[:], ACT.Copy, scale=1.0 / I, accum_out=mean[:])
-        nc.vector.reciprocal(gain[:], mean[:])
+        nc.gpsimd.tensor_tensor(gain[:], mean[:], minus_one[:], ALU.pow)
 
         decayed = []
         for c in range(2):

@@ -68,45 +68,51 @@ def tile_attend_heavyhitter_kernel(tc, query, keys_words, keys_scales, mass, dec
         q_codes = sb.tile([P, Q], U32, name="q_codes", align_bytes=64)
         q_scales = sb.tile([P, Q], U8, name="q_scales", align_bytes=64)
 
-        lists = [offsets[:, h * (HALF // 16) : (h + 1) * (HALF // 16)] for h in range(2)]
+        parts = [(0, LEAD), (LEAD, HALF), (HALF, I)]
         banks = []
         for h in range(2):
             k_scales = sb.tile([P, HALF], U8, name="k_scales%d" % h, align_bytes=64)
-            nc.vector.tensor_copy(k_scales[:], pool_scales[:].indirect(lists[h]))
+            nc.vector.tensor_copy(k_scales[:], pool_scales[:].indirect(offsets[:, h * HALF // 16 : (h + 1) * HALF // 16]))
             if h == 0:
                 nc.vector.quantize_mx(
                     out=q_codes[:].bitcast(FP8X4), scales=q_scales[:], in_=q_grouped[:].rearrange("p h t -> p (h t)")
                 )
-            bank = ps.tile([P, HALF], F32, name="bank%d" % h)
-            nc.tensor.matmul_mx(
-                out=bank[:],
-                lhsT=q_codes[:].bitcast(FP8X4),
-                lhsT_scale=q_scales[:],
-                rhs=k_words[:, h * HALF : (h + 1) * HALF].bitcast(FP4X4),
-                rhs_scale=k_scales[:],
-                start=True,
-                stop=True,
-            )
-            banks.append(bank)
+            for lo, hi in parts:
+                if lo // HALF == h:
+                    bank = ps.tile([P, hi - lo], F32, name="bank%d" % lo)
+                    nc.tensor.matmul_mx(
+                        out=bank[:],
+                        lhsT=q_codes[:].bitcast(FP8X4),
+                        lhsT_scale=q_scales[:],
+                        rhs=k_words[:, lo:hi].bitcast(FP4X4),
+                        rhs_scale=k_scales[:, lo - h * HALF : hi - h * HALF],
+                        start=True,
+                        stop=True,
+                    )
+                    banks.append(bank)
 
+        spare = sb.tile([P, LEAD + HALF], F32, name="spare")
         first = sb.tile([P, 1], F32, name="first")
-        nc.vector.tensor_reduce(out=first[:], in_=banks[0][:], axis=mybir.AxisListType.X, op=ALU.min)
-        spare = sb.tile([P, HALF], F32, name="spare")
+        middle = sb.tile([P, 1], F32, name="middle")
         second = sb.tile([P, 1], F32, name="second")
         nc.vector.tensor_scalar(
-            out=spare[:], in0=banks[1][:], scalar1=HEADROOM, scalar2=first[:], op0=ALU.add, op1=ALU.min,
+            out=spare[:, :LEAD], in0=banks[0][:], scalar1=-HEADROOM, scalar2=None, op0=ALU.add, op1=ALU.min,
+            accum_out=first[:],
+        )
+        nc.vector.tensor_reduce(out=middle[:], in_=banks[1][:], axis=mybir.AxisListType.X, op=ALU.min)
+        nc.vector.tensor_scalar(
+            out=spare[:, LEAD:], in0=banks[2][:], scalar1=first[:], scalar2=middle[:], op0=ALU.min, op1=ALU.min,
             accum_out=second[:],
         )
+
         terms = sb.tile([P, I], F32, name="terms")
         sums = sb.tile([P, 3], F32, name="sums")
-        nc.scalar.activation(
-            terms[:, :LEAD], banks[0][:, :LEAD], ACT.Exp, bias=first[:], scale=-1.0, accum_out=sums[:, 0:1]
-        )
+        for n, (lo, hi) in enumerate(parts):
+            nc.scalar.activation(
+                terms[:, lo:hi], banks[n][:], ACT.Exp, bias=second[:] if n else first[:], scale=-1.0,
+                accum_out=sums[:, n : n + 1],
+            )
         nc.vector.tensor_tensor(window[:].indirect(offsets[:, : LEAD // 16]), terms[:, :LEAD], zeros[:], ALU.add)
-        nc.scalar.activation(
-            terms[:, LEAD:HALF], banks[0][:, LEAD:], ACT.Exp, bias=first[:], scale=-1.0, accum_out=sums[:, 1:2]
-        )
-        nc.scalar.activation(terms[:, HALF:], banks[1][:], ACT.Exp, bias=second[:], scale=-1.0, accum_out=sums[:, 2:3])
         nc.vector.tensor_copy(window[:].indirect(offsets[:, LEAD // 16 :]), terms[:, LEAD:])
         shares = sb.tile([P, 3], F32, name="shares")
         mean = sb.tile([P, 1], F32, name="mean")

@@ -32,16 +32,16 @@ def tile_attend_heavyhitter_kernel(tc, query, keys_words, keys_scales, mass, dec
 
         offsets = sb.tile([P, I // 16], U16, name="offsets")
         pool_words = sb.tile([P, T], U16, name="pool_words", align_bytes=64)
-        pool_scales = sb.tile([P, T], U8, name="pool_scales", align_bytes=64)
-        q_raw = sb.tile([P, PACK, Q], F32, name="q_raw", tag="raw")
+        pool_scales = sb.tile([P, T], U8, name="pool_scales", tag="late", align_bytes=64)
+        q_raw = sb.tile([P, PACK, Q], F32, name="q_raw", tag="raw", align_bytes=64)
         window = sb.tile([P, T], F32, name="window")
 
         nc.vector.memset(pool_scales[:].bitcast(I32), 0)
-        nc.sync.dma_start(out=pool_words[:].bitcast(I32), in_=keys_words[0].bitcast(I32))
-        nc.sync.dma_start(offsets[:], offs)
         nc.sync.dma_start(out=q_raw[:], in_=query.rearrange("(p j) h -> p j h", j=PACK))
+        nc.sync.dma_start(offsets[:], offs)
         for r in range(4):
             nc.sync.dma_start(out=pool_scales[r:P:32, :].bitcast(I32), in_=keys_scales[0, r:16:4, :].bitcast(I32))
+        nc.sync.dma_start(out=pool_words[:].bitcast(I32), in_=keys_words[0].bitcast(I32))
         nc.vector.memset(window[:], 0.0)
         zeros = sb.tile([P, LEAD], F32, name="zeros")
         nc.vector.memset(zeros[:], 0.0)
@@ -50,33 +50,33 @@ def tile_attend_heavyhitter_kernel(tc, query, keys_words, keys_scales, mass, dec
         nc.gpsimd.memset(minus_one[:], -1.0)
 
         q_grouped = sb.tile([P, Q, PACK], BF16, name="q_grouped", align_bytes=64)
-        nc.scalar.activation(
-            q_grouped[:].rearrange("p (c i) t -> p c t i", i=4),
-            q_raw[:].rearrange("p t (c i) -> p c t i", i=4),
-            ACT.Copy,
-            scale=-1.0,
+        nc.vector.tensor_scalar(
+            out=q_grouped[:].rearrange("p (c i) t -> p c t i", i=4),
+            in0=q_raw[:].rearrange("p t (c i) -> p c t i", i=4),
+            scalar1=-1.0,
+            scalar2=None,
+            op0=ALU.mult,
         )
-        old = sb.tile([P, T + 8], F32, name="old", tag="raw")
+        q_codes = sb.tile([P, Q], U32, name="q_codes", align_bytes=64)
+        q_scales = sb.tile([P, Q], U8, name="q_scales", align_bytes=64)
+        nc.vector.quantize_mx(
+            out=q_codes[:].bitcast(FP8X4), scales=q_scales[:], in_=q_grouped[:].rearrange("p h t -> p (h t)")
+        )
+        k_scales = sb.tile([P, I], U8, name="k_scales", tag="raw", align_bytes=64)
+        nc.vector.tensor_copy(k_scales[:], pool_scales[:].indirect(offsets[:]))
+
+        old = sb.tile([P, T + 8], F32, name="old", tag="late", align_bytes=64)
         decay = old[:, T : T + 1]
         nc.sync.dma_start(out=decay, in_=dec)
         for c in range(2):
             cols = slice(c * (T // 2), (c + 1) * (T // 2))
             nc.sync.dma_start(out=old[:, cols], in_=mass[:, cols])
 
-        k_words = sb.tile([P, I], U16, name="k_words", align_bytes=64)
-        nc.vector.tensor_copy(k_words[:], pool_words[:].indirect(offsets[:]))
-        q_codes = sb.tile([P, Q], U32, name="q_codes", align_bytes=64)
-        q_scales = sb.tile([P, Q], U8, name="q_scales", align_bytes=64)
-
         parts = [(0, LEAD), (LEAD, HALF), (HALF, I)]
         banks = []
         for h in range(2):
-            k_scales = sb.tile([P, HALF], U8, name="k_scales%d" % h, align_bytes=64)
-            nc.vector.tensor_copy(k_scales[:], pool_scales[:].indirect(offsets[:, h * HALF // 16 : (h + 1) * HALF // 16]))
-            if h == 0:
-                nc.vector.quantize_mx(
-                    out=q_codes[:].bitcast(FP8X4), scales=q_scales[:], in_=q_grouped[:].rearrange("p h t -> p (h t)")
-                )
+            k_words = sb.tile([P, HALF], U16, name="k_words%d" % h, align_bytes=64)
+            nc.vector.tensor_copy(k_words[:], pool_words[:].indirect(offsets[:, h * HALF // 16 : (h + 1) * HALF // 16]))
             for lo, hi in parts:
                 if lo // HALF == h:
                     bank = ps.tile([P, hi - lo], F32, name="bank%d" % lo)
@@ -84,8 +84,8 @@ def tile_attend_heavyhitter_kernel(tc, query, keys_words, keys_scales, mass, dec
                         out=bank[:],
                         lhsT=q_codes[:].bitcast(FP8X4),
                         lhsT_scale=q_scales[:],
-                        rhs=k_words[:, lo:hi].bitcast(FP4X4),
-                        rhs_scale=k_scales[:, lo - h * HALF : hi - h * HALF],
+                        rhs=k_words[:, lo - h * HALF : hi - h * HALF].bitcast(FP4X4),
+                        rhs_scale=k_scales[:, lo:hi],
                         start=True,
                         stop=True,
                     )

@@ -19,22 +19,23 @@ ACT = mybir.ActivationFunctionType
 P = 128
 PACK = 4
 HALF = I // 2
-LEAD = 128
-HEADROOM = 32.0
-OUT_WIDTHS = (128, 256, 256, 384, 512, 512)
+VECTOR_SLOTS = 128
+HEADROOM = 24.0
+LEAD = 384
 
 
 def tile_attend_heavyhitter_kernel(tc, query, keys_words, keys_scales, mass, dec, offs, out):
     nc = tc.nc
     with ExitStack() as ctx:
         sb = ctx.enter_context(tc.tile_pool(name="sb", bufs=1))
+        shared = ctx.enter_context(tc.tile_pool(name="shared", bufs=1))
         ps = ctx.enter_context(tc.psum_pool(name="ps", bufs=1))
 
         offsets = sb.tile([P, I // 16], U16, name="offsets")
         pool_words = sb.tile([P, T], U16, name="pool_words", align_bytes=64)
-        pool_scales = sb.tile([P, T], U8, name="pool_scales", tag="late", align_bytes=64)
-        q_raw = sb.tile([P, PACK, Q], F32, name="q_raw", tag="raw", align_bytes=64)
-        window = sb.tile([P, T], F32, name="window")
+        pool_scales = sb.tile([P, T], U8, name="pool_scales", align_bytes=64)
+        q_raw = shared.tile([P, PACK, Q], F32, name="q_raw", offset=0, align_bytes=64)
+        window_v = sb.tile([P, T], F32, name="window_v")
 
         nc.vector.memset(pool_scales[:].bitcast(I32), 0)
         nc.sync.dma_start(out=q_raw[:], in_=query.rearrange("(p j) h -> p j h", j=PACK))
@@ -42,14 +43,11 @@ def tile_attend_heavyhitter_kernel(tc, query, keys_words, keys_scales, mass, dec
         for r in range(4):
             nc.sync.dma_start(out=pool_scales[r:P:32, :].bitcast(I32), in_=keys_scales[0, r:16:4, :].bitcast(I32))
         nc.sync.dma_start(out=pool_words[:].bitcast(I32), in_=keys_words[0].bitcast(I32))
-        nc.vector.memset(window[:], 0.0)
-        zeros = sb.tile([P, LEAD], F32, name="zeros")
+        nc.vector.memset(window_v[:], 0.0)
+        zeros = sb.tile([P, VECTOR_SLOTS], F32, name="zeros")
         nc.vector.memset(zeros[:], 0.0)
 
-        minus_one = sb.tile([P, 1], F32, name="minus_one")
-        nc.gpsimd.memset(minus_one[:], -1.0)
-
-        q_grouped = sb.tile([P, Q, PACK], BF16, name="q_grouped", align_bytes=64)
+        q_grouped = sb.tile([P, Q, PACK], BF16, name="q_grouped", tag="reused", align_bytes=64)
         nc.vector.tensor_scalar(
             out=q_grouped[:].rearrange("p (c i) t -> p c t i", i=4),
             in0=q_raw[:].rearrange("p t (c i) -> p c t i", i=4),
@@ -62,17 +60,28 @@ def tile_attend_heavyhitter_kernel(tc, query, keys_words, keys_scales, mass, dec
         nc.vector.quantize_mx(
             out=q_codes[:].bitcast(FP8X4), scales=q_scales[:], in_=q_grouped[:].rearrange("p h t -> p (h t)")
         )
-        k_scales = sb.tile([P, I], U8, name="k_scales", tag="raw", align_bytes=64)
+        k_scales = shared.tile([P, I], U8, name="k_scales", offset=0, align_bytes=64)
         nc.vector.tensor_copy(k_scales[:], pool_scales[:].indirect(offsets[:]))
 
-        old = sb.tile([P, T + 8], F32, name="old", tag="late", align_bytes=64)
+        window_s = sb.tile([P, T], F32, name="window_s", tag="reused", align_bytes=64)
+        nc.gpsimd.memset(window_s[:], 0.0)
+
+        lead = LEAD
+        old = sb.tile([P, T + 8], F32, name="old")
         decay = old[:, T : T + 1]
         nc.sync.dma_start(out=decay, in_=dec)
-        for c in range(2):
-            cols = slice(c * (T // 2), (c + 1) * (T // 2))
-            nc.sync.dma_start(out=old[:, cols], in_=mass[:, cols])
+        for lo, hi in ((0, T // 2), (T // 2, T)):
+            nc.sync.dma_start(out=old[:, lo:hi], in_=mass[:, lo:hi])
+        decay_share = sb.tile([P, 1], F32, name="decay_share")
+        nc.gpsimd.tensor_scalar(
+            out=decay_share[:], in0=decay, scalar1=1.0 / I, scalar2=0.0, op0=ALU.mult, op1=ALU.add
+        )
+        decayed = sb.tile([P, lead], F32, name="decayed")
+        nc.gpsimd.tensor_scalar(
+            out=decayed[:], in0=old[:, :lead], scalar1=decay, scalar2=0.0, op0=ALU.mult, op1=ALU.add
+        )
 
-        parts = [(0, LEAD), (LEAD, HALF), (HALF, I)]
+        parts = ((0, HALF), (HALF, I))
         banks = []
         for h in range(2):
             k_words = sb.tile([P, HALF], U16, name="k_words%d" % h, align_bytes=64)
@@ -91,52 +100,73 @@ def tile_attend_heavyhitter_kernel(tc, query, keys_words, keys_scales, mass, dec
                     )
                     banks.append(bank)
 
-        spare = sb.tile([P, LEAD + HALF], F32, name="spare")
-        first = sb.tile([P, 1], F32, name="first")
-        middle = sb.tile([P, 1], F32, name="middle")
-        second = sb.tile([P, 1], F32, name="second")
-        nc.vector.tensor_scalar(
-            out=spare[:, :LEAD], in0=banks[0][:], scalar1=-HEADROOM, scalar2=None, op0=ALU.add, op1=ALU.min,
-            accum_out=first[:],
-        )
-        nc.vector.tensor_reduce(out=middle[:], in_=banks[1][:], axis=mybir.AxisListType.X, op=ALU.min)
-        nc.vector.tensor_scalar(
-            out=spare[:, LEAD:], in0=banks[2][:], scalar1=first[:], scalar2=middle[:], op0=ALU.min, op1=ALU.min,
-            accum_out=second[:],
-        )
-
+        spare = sb.tile([P, HALF], F32, name="spare")
         terms = sb.tile([P, I], F32, name="terms")
-        sums = sb.tile([P, 3], F32, name="sums")
+        sums = sb.tile([P, len(parts)], F32, name="sums")
+        shifts = [sb.tile([P, 1], F32, name="shift%d" % n) for n in range(len(parts))]
+        nc.vector.tensor_reduce(out=shifts[0][:], in_=banks[0][:], axis=mybir.AxisListType.X, op=ALU.min)
+        for n in range(1, len(parts)):
+            lo, hi = parts[n]
+            nc.vector.tensor_scalar(
+                out=spare[:, lo - HALF : hi - HALF], in0=banks[n][:], scalar1=n * HEADROOM, scalar2=shifts[n - 1][:],
+                op0=ALU.add, op1=ALU.min, accum_out=shifts[n][:],
+            )
         for n, (lo, hi) in enumerate(parts):
             nc.scalar.activation(
-                terms[:, lo:hi], banks[n][:], ACT.Exp, bias=second[:] if n else first[:], scale=-1.0,
-                accum_out=sums[:, n : n + 1],
+                terms[:, lo:hi], banks[n][:], ACT.Exp, bias=shifts[n][:], scale=-1.0, accum_out=sums[:, n : n + 1]
             )
-        nc.vector.tensor_tensor(window[:].indirect(offsets[:, : LEAD // 16]), terms[:, :LEAD], zeros[:], ALU.add)
-        nc.vector.tensor_copy(window[:].indirect(offsets[:, LEAD // 16 :]), terms[:, LEAD:])
-        shares = sb.tile([P, 3], F32, name="shares")
+        nc.vector.tensor_tensor(
+            window_v[:].indirect(offsets[:, : VECTOR_SLOTS // 16]), terms[:, :VECTOR_SLOTS], zeros[:], ALU.add
+        )
+        nc.scalar.activation(window_s[:].indirect(offsets[:, VECTOR_SLOTS // 16 :]), terms[:, VECTOR_SLOTS:], ACT.Copy)
+
+        scaled_sums = sb.tile([P, 2, len(parts)], F32, name="scaled_sums")
+        carry = sb.tile([P, 1], F32, name="carry")
         mean = sb.tile([P, 1], F32, name="mean")
         gain = sb.tile([P, 1], F32, name="gain")
-        nc.scalar.activation(shares[:], sums[:], ACT.Copy, scale=1.0 / I, accum_out=mean[:])
-        nc.gpsimd.tensor_tensor(gain[:], mean[:], minus_one[:], ALU.pow)
+        nc.vector.tensor_scalar(
+            out=scaled_sums[:, 0, :], in0=sums[:], scalar1=1.0 / I, scalar2=None, op0=ALU.mult, op1=ALU.add,
+            accum_out=mean[:],
+        )
+        nc.vector.tensor_scalar(
+            out=scaled_sums[:, 1, :], in0=sums[:], scalar1=decay_share[:], scalar2=None, op0=ALU.mult, op1=ALU.add,
+            accum_out=carry[:],
+        )
+        nc.vector.reciprocal(gain[:], mean[:])
 
-        decayed = []
-        for c in range(2):
-            part = sb.tile([P, T // 2], F32, name="decayed%d" % c)
-            nc.scalar.activation(part[:], old[:, c * (T // 2) : (c + 1) * (T // 2)], ACT.Copy, scale=decay)
-            decayed.append(part)
+        partial = sb.tile([P, T], F32, name="partial")
+        placed = sb.tile([P, T], F32, name="placed")
+        lead_partial = partial[:, :lead]
+        res = sb.tile([P, T], F32, name="res")
 
-        lo = 0
-        for n, width in enumerate(OUT_WIDTHS):
-            res = sb.tile([P, width], F32, name="res%d" % n)
-            done = 0
-            while done < width:
-                c, at = divmod(lo + done, T // 2)
-                take = min(width - done, T // 2 - at)
-                nc.vector.scalar_tensor_tensor(
-                    out=res[:, done : done + take], in0=window[:, lo + done : lo + done + take], scalar=gain[:],
-                    in1=decayed[c][:, at : at + take], op0=ALU.mult, op1=ALU.add,
-                )
-                done = done + take
-            nc.sync.dma_start(out=out[:, lo : lo + width], in_=res[:])
-            lo = lo + width
+        def first_sum(lo, hi, into):
+            nc.vector.scalar_tensor_tensor(
+                out=into, in0=old[:, lo:hi], scalar=carry[:], in1=window_v[:, lo:hi], op0=ALU.mult, op1=ALU.add
+            )
+
+        def second_sum(lo, hi, scaled, added, res):
+            nc.vector.scalar_tensor_tensor(out=res, in0=scaled, scalar=gain[:], in1=added, op0=ALU.mult, op1=ALU.add)
+
+        def store(lo, hi):
+            nc.sync.dma_start(out=out[:, lo:hi], in_=res[:, lo:hi])
+
+        for lo, hi in ((384, 640), (640, 896), (896, 1408), (1408, 1664), (1664, 2048)):
+            nc.scalar.activation(placed[:, lo:hi], window_s[:, lo:hi], ACT.Copy, scale=gain[:])
+
+        first_sum(384, 1024, partial[:, 384:1024])
+        nc.vector.scalar_tensor_tensor(
+            out=lead_partial, in0=window_v[:, :lead], scalar=gain[:], in1=decayed[:], op0=ALU.mult, op1=ALU.add
+        )
+        first_sum(1024, 1664, partial[:, 1024:1664])
+        for lo, hi in ((0, 128), (128, 384)):
+            second_sum(lo, hi, window_s[:, lo:hi], lead_partial[:, lo:hi], res[:, lo:hi])
+            store(lo, hi)
+        for lo, hi in ((384, 640), (640, 896)):
+            second_sum(lo, hi, partial[:, lo:hi], placed[:, lo:hi], res[:, lo:hi])
+        store(384, 896)
+        second_sum(896, 1408, partial[:, 896:1408], placed[:, 896:1408], res[:, 896:1408])
+        store(896, 1408)
+        first_sum(1664, 2048, partial[:, 1664:2048])
+        for lo, hi in ((1408, 1664), (1664, 2048)):
+            second_sum(lo, hi, partial[:, lo:hi], placed[:, lo:hi], res[:, lo:hi])
+            store(lo, hi)

@@ -120,19 +120,15 @@ def tile_attend_heavyhitter_kernel(tc, query, keys_words, keys_scales, mass, dec
         )
         nc.scalar.activation(window_s[:].indirect(offsets[:, VECTOR_SLOTS // 16 :]), terms[:, VECTOR_SLOTS:], ACT.Copy)
 
-        scaled_sums = sb.tile([P, 2, len(parts)], F32, name="scaled_sums")
         carry = sb.tile([P, 1], F32, name="carry")
         mean = sb.tile([P, 1], F32, name="mean")
         gain = sb.tile([P, 1], F32, name="gain")
         nc.vector.tensor_scalar(
-            out=scaled_sums[:, 0, :], in0=sums[:], scalar1=1.0 / I, scalar2=None, op0=ALU.mult, op1=ALU.add,
-            accum_out=mean[:],
+            out=carry[:], in0=sums[:, 0:1], scalar1=sums[:, 1:2], scalar2=decay_share[:], op0=ALU.add, op1=ALU.mult
         )
         nc.vector.tensor_scalar(
-            out=scaled_sums[:, 1, :], in0=sums[:], scalar1=decay_share[:], scalar2=None, op0=ALU.mult, op1=ALU.add,
-            accum_out=carry[:],
+            out=mean[:], in0=sums[:, 0:1], scalar1=sums[:, 1:2], scalar2=1.0 / I, op0=ALU.add, op1=ALU.mult
         )
-        nc.vector.reciprocal(gain[:], mean[:])
 
         partial = sb.tile([P, T], F32, name="partial")
         placed = sb.tile([P, T], F32, name="placed")
@@ -150,23 +146,21 @@ def tile_attend_heavyhitter_kernel(tc, query, keys_words, keys_scales, mass, dec
         def store(lo, hi):
             nc.sync.dma_start(out=out[:, lo:hi], in_=res[:, lo:hi])
 
-        for lo, hi in ((384, 640), (640, 896), (896, 1408), (1408, 1664), (1664, 2048)):
-            nc.scalar.activation(placed[:, lo:hi], window_s[:, lo:hi], ACT.Copy, scale=gain[:])
-
-        first_sum(384, 1024, partial[:, 384:1024])
+        edges = (0, 128, 384, 640, 1024, 1536, 2048)
+        pieces = list(zip(edges[:-1], edges[1:]))
+        first_sum(384, 704, partial[:, 384:704])
+        nc.vector.reciprocal(gain[:], mean[:])
+        first_sum(704, 1024, partial[:, 704:1024])
         nc.vector.scalar_tensor_tensor(
             out=lead_partial, in0=window_v[:, :lead], scalar=gain[:], in1=decayed[:], op0=ALU.mult, op1=ALU.add
         )
-        first_sum(1024, 1664, partial[:, 1024:1664])
-        for lo, hi in ((0, 128), (128, 384)):
-            second_sum(lo, hi, window_s[:, lo:hi], lead_partial[:, lo:hi], res[:, lo:hi])
-            store(lo, hi)
-        for lo, hi in ((384, 640), (640, 896)):
-            second_sum(lo, hi, partial[:, lo:hi], placed[:, lo:hi], res[:, lo:hi])
-        store(384, 896)
-        second_sum(896, 1408, partial[:, 896:1408], placed[:, 896:1408], res[:, 896:1408])
-        store(896, 1408)
-        first_sum(1664, 2048, partial[:, 1664:2048])
-        for lo, hi in ((1408, 1664), (1664, 2048)):
-            second_sum(lo, hi, partial[:, lo:hi], placed[:, lo:hi], res[:, lo:hi])
+        first_sum(1024, 2048, partial[:, 1024:2048])
+        for lo, hi in pieces[2:]:
+            nc.scalar.activation(placed[:, lo:hi], window_s[:, lo:hi], ACT.Copy, scale=gain[:])
+
+        for lo, hi in pieces:
+            if hi <= lead:
+                second_sum(lo, hi, window_s[:, lo:hi], lead_partial[:, lo:hi], res[:, lo:hi])
+            else:
+                second_sum(lo, hi, partial[:, lo:hi], placed[:, lo:hi], res[:, lo:hi])
             store(lo, hi)

@@ -19,9 +19,9 @@ ACT = mybir.ActivationFunctionType
 P = 128
 PACK = 4
 HALF = I // 2
-VECTOR_SLOTS = 128
+VECTOR_SLOTS = 160
 HEADROOM = 24.0
-LEAD = 384
+LEAD = 640
 
 
 def tile_attend_heavyhitter_kernel(tc, query, keys_words, keys_scales, mass, dec, offs, out):
@@ -67,10 +67,10 @@ def tile_attend_heavyhitter_kernel(tc, query, keys_words, keys_scales, mass, dec
         nc.gpsimd.memset(window_s[:], 0.0)
 
         lead = LEAD
-        old = sb.tile([P, T + 8], F32, name="old")
+        old = shared.tile([P, T + 8], F32, name="old", offset=I, align_bytes=64)
         decay = old[:, T : T + 1]
         nc.sync.dma_start(out=decay, in_=dec)
-        for lo, hi in ((0, T // 2), (T // 2, T)):
+        for lo, hi in ((0, lead), (lead, T)):
             nc.sync.dma_start(out=old[:, lo:hi], in_=mass[:, lo:hi])
         decay_share = sb.tile([P, 1], F32, name="decay_share")
         nc.gpsimd.tensor_scalar(
@@ -122,7 +122,7 @@ def tile_attend_heavyhitter_kernel(tc, query, keys_words, keys_scales, mass, dec
 
         carry = sb.tile([P, 1], F32, name="carry")
         mean = sb.tile([P, 1], F32, name="mean")
-        gain = sb.tile([P, 1], F32, name="gain")
+        gain = old[:, lead : lead + 1]
         nc.vector.tensor_scalar(
             out=carry[:], in0=sums[:, 0:1], scalar1=sums[:, 1:2], scalar2=decay_share[:], op0=ALU.add, op1=ALU.mult
         )
@@ -141,22 +141,23 @@ def tile_attend_heavyhitter_kernel(tc, query, keys_words, keys_scales, mass, dec
             )
 
         def second_sum(lo, hi, scaled, added, res):
-            nc.vector.scalar_tensor_tensor(out=res, in0=scaled, scalar=gain[:], in1=added, op0=ALU.mult, op1=ALU.add)
+            nc.vector.scalar_tensor_tensor(out=res, in0=scaled, scalar=gain, in1=added, op0=ALU.mult, op1=ALU.add)
 
         def store(lo, hi):
             nc.sync.dma_start(out=out[:, lo:hi], in_=res[:, lo:hi])
 
         edges = (0, 128, 384, 640, 1024, 1536, 2048)
         pieces = list(zip(edges[:-1], edges[1:]))
-        first_sum(384, 704, partial[:, 384:704])
-        nc.vector.reciprocal(gain[:], mean[:])
-        first_sum(704, 1024, partial[:, 704:1024])
+        first_sum(640, 768, partial[:, 640:768])
+        first_sum(768, 1216, partial[:, 768:1216])
+        nc.vector.reciprocal(gain, mean[:])
+        first_sum(1216, 1600, partial[:, 1216:1600])
         nc.vector.scalar_tensor_tensor(
-            out=lead_partial, in0=window_v[:, :lead], scalar=gain[:], in1=decayed[:], op0=ALU.mult, op1=ALU.add
+            out=lead_partial, in0=window_v[:, :lead], scalar=gain, in1=decayed[:], op0=ALU.mult, op1=ALU.add
         )
-        first_sum(1024, 2048, partial[:, 1024:2048])
-        for lo, hi in pieces[2:]:
-            nc.scalar.activation(placed[:, lo:hi], window_s[:, lo:hi], ACT.Copy, scale=gain[:])
+        first_sum(1600, 2048, partial[:, 1600:2048])
+        for lo, hi in pieces[3:]:
+            nc.scalar.activation(placed[:, lo:hi], window_s[:, lo:hi], ACT.Copy, scale=gain)
 
         for lo, hi in pieces:
             if hi <= lead:

@@ -19,7 +19,7 @@ ACT = mybir.ActivationFunctionType
 P = 128
 PACK = 4
 HALF = I // 2
-VECTOR_SLOTS = 160
+VECTOR_SLOTS = 192
 HEADROOM = 24.0
 LEAD = 640
 
@@ -148,20 +148,24 @@ def tile_attend_heavyhitter_kernel(tc, query, keys_words, keys_scales, mass, dec
 
         edges = (0, 128, 384, 640, 1024, 1536, 2048)
         pieces = list(zip(edges[:-1], edges[1:]))
-        first_sum(640, 768, partial[:, 640:768])
-        first_sum(768, 1216, partial[:, 768:1216])
+        first_sum(640, 704, partial[:, 640:704])
+        first_sum(704, 1088, partial[:, 704:1088])
         nc.vector.reciprocal(gain, mean[:])
-        first_sum(1216, 1600, partial[:, 1216:1600])
+        first_sum(1088, 1472, partial[:, 1088:1472])
         nc.vector.scalar_tensor_tensor(
             out=lead_partial, in0=window_v[:, :lead], scalar=gain, in1=decayed[:], op0=ALU.mult, op1=ALU.add
         )
-        first_sum(1600, 2048, partial[:, 1600:2048])
+        first_sum(1472, 1856, partial[:, 1472:1856])
         for lo, hi in pieces[3:]:
             nc.scalar.activation(placed[:, lo:hi], window_s[:, lo:hi], ACT.Copy, scale=gain)
 
-        for lo, hi in pieces:
+        for lo, hi in pieces[:-1]:
             if hi <= lead:
                 second_sum(lo, hi, window_s[:, lo:hi], lead_partial[:, lo:hi], res[:, lo:hi])
             else:
                 second_sum(lo, hi, partial[:, lo:hi], placed[:, lo:hi], res[:, lo:hi])
             store(lo, hi)
+        first_sum(1856, 2048, partial[:, 1856:2048])
+        for lo, hi in ((1536, 1856), (1856, 2048)):
+            second_sum(lo, hi, partial[:, lo:hi], placed[:, lo:hi], res[:, lo:hi])
+        store(1536, 2048)

@@ -148,24 +148,28 @@ def tile_attend_heavyhitter_kernel(tc, query, keys_words, keys_scales, mass, dec
 
         edges = (0, 128, 384, 640, 1024, 1536, 2048)
         pieces = list(zip(edges[:-1], edges[1:]))
-        first_sum(640, 704, partial[:, 640:704])
-        first_sum(704, 1088, partial[:, 704:1088])
+        first_sum(640, 672, partial[:, 640:672])
+        first_sum(672, 1056, partial[:, 672:1056])
         nc.vector.reciprocal(gain, mean[:])
-        first_sum(1088, 1472, partial[:, 1088:1472])
-        nc.vector.scalar_tensor_tensor(
-            out=lead_partial, in0=window_v[:, :lead], scalar=gain, in1=decayed[:], op0=ALU.mult, op1=ALU.add
-        )
-        first_sum(1472, 1856, partial[:, 1472:1856])
+        first_sum(1056, 1440, partial[:, 1056:1440])
+        for lo, hi in ((0, 384), (384, lead)):
+            nc.vector.scalar_tensor_tensor(
+                out=lead_partial[:, lo:hi], in0=window_v[:, lo:hi], scalar=gain, in1=decayed[:, lo:hi],
+                op0=ALU.mult, op1=ALU.add,
+            )
+        first_sum(1440, 1568, partial[:, 1440:1568])
         for lo, hi in pieces[3:]:
             nc.scalar.activation(placed[:, lo:hi], window_s[:, lo:hi], ACT.Copy, scale=gain)
 
         for lo, hi in pieces[:-1]:
+            if lo == 1024:
+                first_sum(1568, 1808, partial[:, 1568:1808])
             if hi <= lead:
                 second_sum(lo, hi, window_s[:, lo:hi], lead_partial[:, lo:hi], res[:, lo:hi])
             else:
                 second_sum(lo, hi, partial[:, lo:hi], placed[:, lo:hi], res[:, lo:hi])
             store(lo, hi)
-        first_sum(1856, 2048, partial[:, 1856:2048])
-        for lo, hi in ((1536, 1856), (1856, 2048)):
+        first_sum(1808, 2048, partial[:, 1808:2048])
+        for lo, hi in ((1536, 1808), (1808, 2048)):
             second_sum(lo, hi, partial[:, lo:hi], placed[:, lo:hi], res[:, lo:hi])
         store(1536, 2048)

@@ -1,6 +1,7 @@
 from contextlib import ExitStack
 
 import concourse.mybir as mybir
+from concourse.masks import make_identity
 
 D, T, I, Q = 512, 2048, 512, 128
 FLOPS = 2 * D * I * Q
@@ -19,9 +20,10 @@ ACT = mybir.ActivationFunctionType
 P = 128
 PACK = 4
 HALF = I // 2
-VECTOR_SLOTS = 192
 HEADROOM = 24.0
-LEAD = 640
+DECAYED = 1024
+TURNED = 384
+EARLY = 768
 
 
 def tile_attend_heavyhitter_kernel(tc, query, keys_words, keys_scales, mass, dec, offs, out):
@@ -33,7 +35,7 @@ def tile_attend_heavyhitter_kernel(tc, query, keys_words, keys_scales, mass, dec
 
         offsets = sb.tile([P, I // 16], U16, name="offsets")
         pool_words = sb.tile([P, T], U16, name="pool_words", align_bytes=64)
-        pool_scales = sb.tile([P, T], U8, name="pool_scales", align_bytes=64)
+        pool_scales = sb.tile([P, T], U8, name="pool_scales", tag="scales_then_identity", align_bytes=64)
         q_raw = shared.tile([P, PACK, Q], F32, name="q_raw", offset=0, align_bytes=64)
         window_v = sb.tile([P, T], F32, name="window_v")
 
@@ -44,10 +46,10 @@ def tile_attend_heavyhitter_kernel(tc, query, keys_words, keys_scales, mass, dec
             nc.sync.dma_start(out=pool_scales[r:P:32, :].bitcast(I32), in_=keys_scales[0, r:16:4, :].bitcast(I32))
         nc.sync.dma_start(out=pool_words[:].bitcast(I32), in_=keys_words[0].bitcast(I32))
         nc.vector.memset(window_v[:], 0.0)
-        zeros = sb.tile([P, VECTOR_SLOTS], F32, name="zeros")
-        nc.vector.memset(zeros[:], 0.0)
+        minus_one = sb.tile([P, 1], F32, name="minus_one")
+        nc.vector.memset(minus_one[:], -1.0)
 
-        q_grouped = sb.tile([P, Q, PACK], BF16, name="q_grouped", tag="reused", align_bytes=64)
+        q_grouped = sb.tile([P, Q, PACK], BF16, name="q_grouped", tag="queries_then_window", align_bytes=64)
         nc.vector.tensor_scalar(
             out=q_grouped[:].rearrange("p (c i) t -> p c t i", i=4),
             in0=q_raw[:].rearrange("p t (c i) -> p c t i", i=4),
@@ -63,113 +65,137 @@ def tile_attend_heavyhitter_kernel(tc, query, keys_words, keys_scales, mass, dec
         k_scales = shared.tile([P, I], U8, name="k_scales", offset=0, align_bytes=64)
         nc.vector.tensor_copy(k_scales[:], pool_scales[:].indirect(offsets[:]))
 
-        window_s = sb.tile([P, T], F32, name="window_s", tag="reused", align_bytes=64)
+        window_s = sb.tile([P, T], F32, name="window_s", tag="queries_then_window", align_bytes=64)
         nc.gpsimd.memset(window_s[:], 0.0)
 
-        lead = LEAD
         old = shared.tile([P, T + 8], F32, name="old", offset=I, align_bytes=64)
         decay = old[:, T : T + 1]
         nc.sync.dma_start(out=decay, in_=dec)
-        for lo, hi in ((0, lead), (lead, T)):
+        for lo, hi in ((0, DECAYED), (DECAYED, T)):
             nc.sync.dma_start(out=old[:, lo:hi], in_=mass[:, lo:hi])
+        identity = sb.tile([P, P], F32, name="identity", tag="scales_then_identity", align_bytes=64)
+        make_identity(nc, identity[:])
         decay_share = sb.tile([P, 1], F32, name="decay_share")
         nc.gpsimd.tensor_scalar(
             out=decay_share[:], in0=decay, scalar1=1.0 / I, scalar2=0.0, op0=ALU.mult, op1=ALU.add
         )
-        decayed = sb.tile([P, lead], F32, name="decayed")
+        decayed = sb.tile([P, DECAYED], F32, name="decayed")
         nc.gpsimd.tensor_scalar(
-            out=decayed[:], in0=old[:, :lead], scalar1=decay, scalar2=0.0, op0=ALU.mult, op1=ALU.add
+            out=decayed[:], in0=old[:, :DECAYED], scalar1=decay, scalar2=0.0, op0=ALU.mult, op1=ALU.add
         )
 
-        parts = ((0, HALF), (HALF, I))
         banks = []
         for h in range(2):
             k_words = sb.tile([P, HALF], U16, name="k_words%d" % h, align_bytes=64)
             nc.vector.tensor_copy(k_words[:], pool_words[:].indirect(offsets[:, h * HALF // 16 : (h + 1) * HALF // 16]))
-            for lo, hi in parts:
-                if lo // HALF == h:
-                    bank = ps.tile([P, hi - lo], F32, name="bank%d" % lo)
-                    nc.tensor.matmul_mx(
-                        out=bank[:],
-                        lhsT=q_codes[:].bitcast(FP8X4),
-                        lhsT_scale=q_scales[:],
-                        rhs=k_words[:, lo - h * HALF : hi - h * HALF].bitcast(FP4X4),
-                        rhs_scale=k_scales[:, lo:hi],
-                        start=True,
-                        stop=True,
-                    )
-                    banks.append(bank)
+            bank = ps.tile([P, HALF], F32, name="bank%d" % h)
+            nc.tensor.matmul_mx(
+                out=bank[:],
+                lhsT=q_codes[:].bitcast(FP8X4),
+                lhsT_scale=q_scales[:],
+                rhs=k_words[:].bitcast(FP4X4),
+                rhs_scale=k_scales[:, h * HALF : (h + 1) * HALF],
+                start=True,
+                stop=True,
+            )
+            banks.append(bank)
 
         spare = sb.tile([P, HALF], F32, name="spare")
         terms = sb.tile([P, I], F32, name="terms")
-        sums = sb.tile([P, len(parts)], F32, name="sums")
-        shifts = [sb.tile([P, 1], F32, name="shift%d" % n) for n in range(len(parts))]
+        sums = sb.tile([P, 2], F32, name="sums")
+        shifts = [sb.tile([P, 1], F32, name="shift%d" % n) for n in range(2)]
         nc.vector.tensor_reduce(out=shifts[0][:], in_=banks[0][:], axis=mybir.AxisListType.X, op=ALU.min)
-        for n in range(1, len(parts)):
-            lo, hi = parts[n]
-            nc.vector.tensor_scalar(
-                out=spare[:, lo - HALF : hi - HALF], in0=banks[n][:], scalar1=n * HEADROOM, scalar2=shifts[n - 1][:],
-                op0=ALU.add, op1=ALU.min, accum_out=shifts[n][:],
-            )
-        for n, (lo, hi) in enumerate(parts):
+        nc.vector.tensor_scalar(
+            out=spare[:], in0=banks[1][:], scalar1=HEADROOM, scalar2=shifts[0][:],
+            op0=ALU.add, op1=ALU.min, accum_out=shifts[1][:],
+        )
+        for h in range(2):
             nc.scalar.activation(
-                terms[:, lo:hi], banks[n][:], ACT.Exp, bias=shifts[n][:], scale=-1.0, accum_out=sums[:, n : n + 1]
+                terms[:, h * HALF : (h + 1) * HALF], banks[h][:], ACT.Exp,
+                bias=shifts[h][:], scale=-1.0, accum_out=sums[:, h : h + 1],
             )
-        nc.vector.tensor_tensor(
-            window_v[:].indirect(offsets[:, : VECTOR_SLOTS // 16]), terms[:, :VECTOR_SLOTS], zeros[:], ALU.add
-        )
-        nc.scalar.activation(window_s[:].indirect(offsets[:, VECTOR_SLOTS // 16 :]), terms[:, VECTOR_SLOTS:], ACT.Copy)
+        nc.vector.tensor_copy(window_v[:].indirect(offsets[:, : HALF // 16]), terms[:, :HALF])
+        nc.scalar.activation(window_s[:].indirect(offsets[:, HALF // 16 :]), terms[:, HALF:], ACT.Copy)
 
-        carry = sb.tile([P, 1], F32, name="carry")
         mean = sb.tile([P, 1], F32, name="mean")
-        gain = old[:, lead : lead + 1]
-        nc.vector.tensor_scalar(
-            out=carry[:], in0=sums[:, 0:1], scalar1=sums[:, 1:2], scalar2=decay_share[:], op0=ALU.add, op1=ALU.mult
-        )
-        nc.vector.tensor_scalar(
+        carry = sb.tile([P, 1], F32, name="carry")
+        gain = sb.tile([P, 1], F32, name="gain")
+        nc.gpsimd.tensor_scalar(
             out=mean[:], in0=sums[:, 0:1], scalar1=sums[:, 1:2], scalar2=1.0 / I, op0=ALU.add, op1=ALU.mult
         )
+        nc.gpsimd.tensor_scalar(
+            out=carry[:], in0=sums[:, 0:1], scalar1=sums[:, 1:2], scalar2=decay_share[:], op0=ALU.add, op1=ALU.mult
+        )
+        nc.gpsimd.tensor_tensor(out=gain[:], in0=mean[:], in1=minus_one[:], op=ALU.pow)
 
-        partial = sb.tile([P, T], F32, name="partial")
-        placed = sb.tile([P, T], F32, name="placed")
-        lead_partial = partial[:, :lead]
+        first_turned = T - TURNED
+        carried = sb.tile([P, TURNED], F32, name="carried")
+        nc.vector.tensor_scalar(
+            out=carried[:], in0=old[:, first_turned:T], scalar1=carry[:], scalar2=None, op0=ALU.mult
+        )
+
+        partial = sb.tile([P, first_turned], F32, name="partial")
+        placed = sb.tile([P, first_turned], F32, name="placed")
         res = sb.tile([P, T], F32, name="res")
 
-        def first_sum(lo, hi, into):
+        def first_sum(lo, hi):
+            if hi <= DECAYED:
+                scaled, factor, added = window_v[:, lo:hi], gain[:], decayed[:, lo:hi]
+            else:
+                scaled, factor, added = old[:, lo:hi], carry[:], window_v[:, lo:hi]
             nc.vector.scalar_tensor_tensor(
-                out=into, in0=old[:, lo:hi], scalar=carry[:], in1=window_v[:, lo:hi], op0=ALU.mult, op1=ALU.add
+                out=partial[:, lo:hi], in0=scaled, scalar=factor, in1=added, op0=ALU.mult, op1=ALU.add
             )
 
-        def second_sum(lo, hi, scaled, added, res):
-            nc.vector.scalar_tensor_tensor(out=res, in0=scaled, scalar=gain, in1=added, op0=ALU.mult, op1=ALU.add)
+        def second_sum(lo, hi):
+            if hi <= DECAYED:
+                scaled, added = window_s[:, lo:hi], partial[:, lo:hi]
+            else:
+                scaled, added = partial[:, lo:hi], placed[:, lo:hi]
+            nc.vector.scalar_tensor_tensor(
+                out=res[:, lo:hi], in0=scaled, scalar=gain[:], in1=added, op0=ALU.mult, op1=ALU.add
+            )
 
         def store(lo, hi):
             nc.sync.dma_start(out=out[:, lo:hi], in_=res[:, lo:hi])
 
-        edges = (0, 128, 384, 640, 1024, 1536, 2048)
-        pieces = list(zip(edges[:-1], edges[1:]))
-        first_sum(640, 672, partial[:, 640:672])
-        first_sum(672, 1056, partial[:, 672:1056])
-        nc.vector.reciprocal(gain, mean[:])
-        first_sum(1056, 1440, partial[:, 1056:1440])
-        for lo, hi in ((0, 384), (384, lead)):
-            nc.vector.scalar_tensor_tensor(
-                out=lead_partial[:, lo:hi], in0=window_v[:, lo:hi], scalar=gain, in1=decayed[:, lo:hi],
-                op0=ALU.mult, op1=ALU.add,
-            )
-        first_sum(1440, 1568, partial[:, 1440:1568])
-        for lo, hi in pieces[3:]:
-            nc.scalar.activation(placed[:, lo:hi], window_s[:, lo:hi], ACT.Copy, scale=gain)
+        def turn(bank, source, start, stop):
+            nc.tensor.matmul(bank, lhsT=source, rhs=identity[:], is_transpose=True, start=start, stop=stop)
 
-        for lo, hi in pieces[:-1]:
-            if lo == 1024:
-                first_sum(1568, 1808, partial[:, 1568:1808])
-            if hi <= lead:
-                second_sum(lo, hi, window_s[:, lo:hi], lead_partial[:, lo:hi], res[:, lo:hi])
-            else:
-                second_sum(lo, hi, partial[:, lo:hi], placed[:, lo:hi], res[:, lo:hi])
-            store(lo, hi)
-        first_sum(1808, 2048, partial[:, 1808:2048])
-        for lo, hi in ((1536, 1808), (1808, 2048)):
-            second_sum(lo, hi, partial[:, lo:hi], placed[:, lo:hi], res[:, lo:hi])
-        store(1536, 2048)
+        blocks = range(TURNED // P)
+        summed = [ps.tile([P, P], F32, name="summed%d" % b) for b in blocks]
+        back = [ps.tile([P, P], F32, name="back%d" % b) for b in blocks]
+        staged = [sb.tile([P, P], F32, name="staged%d" % b) for b in blocks]
+        columns = [slice(first_turned + b * P, first_turned + (b + 1) * P) for b in blocks]
+        for b in blocks:
+            turn(summed[b][:], window_v[:, columns[b]], True, False)
+        for b in blocks:
+            turn(summed[b][:], carried[:, b * P : (b + 1) * P], False, False)
+            turn(summed[b][:], window_s[:, columns[b]], False, True)
+        nc.scalar.activation(placed[:, 1024:1344], window_s[:, 1024:1344], ACT.Copy, scale=gain[:])
+        for b in blocks:
+            nc.scalar.copy(staged[b][:], summed[b][:])
+            turn(back[b][:], staged[b][:], True, True)
+        nc.scalar.activation(placed[:, 1344:1664], window_s[:, 1344:1664], ACT.Copy, scale=gain[:])
+        for b in blocks:
+            nc.scalar.activation(res[:, columns[b]], back[b][:], ACT.Copy, scale=gain[:])
+
+        first_sum(0, 384)
+        first_sum(384, EARLY)
+        second_sum(0, 128)
+        store(0, 128)
+        second_sum(128, 384)
+        store(128, 384)
+        second_sum(384, 640)
+        store(384, 640)
+        first_sum(EARLY, 1024)
+        second_sum(640, EARLY)
+        second_sum(EARLY, 1024)
+        store(640, 1024)
+        first_sum(1024, 1344)
+        first_sum(1344, 1664)
+        store(first_turned, T)
+        second_sum(1024, 1344)
+        store(1024, 1344)
+        second_sum(1344, 1664)
+        store(1344, 1664)

@@ -68,17 +68,16 @@ def tile_attend_heavyhitter_kernel(tc, query, keys_words, keys_scales, mass, dec
         window_s = sb.tile([P, T], F32, name="window_s", tag="queries_then_window", align_bytes=64)
         nc.gpsimd.memset(window_s[:], 0.0)
 
-        old = shared.tile([P, T + 8], F32, name="old", offset=I, align_bytes=64)
-        decay = old[:, T : T + 1]
-        nc.sync.dma_start(out=decay, in_=dec)
+        old = shared.tile([P, T], F32, name="old", offset=I, align_bytes=64)
+        decay_tile = sb.tile([P, 1], F32, name="decay_tile")
+        decay = decay_tile[:]
+        nc.gpsimd.dma_start(out=decay, in_=dec)
         for lo, hi in ((0, DECAYED), (DECAYED, T)):
             nc.sync.dma_start(out=old[:, lo:hi], in_=mass[:, lo:hi])
         identity = sb.tile([P, P], F32, name="identity", tag="scales_then_identity", align_bytes=64)
         make_identity(nc, identity[:])
         decay_share = sb.tile([P, 1], F32, name="decay_share")
-        nc.gpsimd.tensor_scalar(
-            out=decay_share[:], in0=decay, scalar1=1.0 / I, scalar2=0.0, op0=ALU.mult, op1=ALU.add
-        )
+        nc.scalar.activation(decay_share[:], decay, ACT.Copy, scale=1.0 / I)
         decayed = sb.tile([P, DECAYED], F32, name="decayed")
         nc.gpsimd.tensor_scalar(
             out=decayed[:], in0=old[:, :DECAYED], scalar1=decay, scalar2=0.0, op0=ALU.mult, op1=ALU.add

@@ -21,9 +21,9 @@ P = 128
 PACK = 4
 HALF = I // 2
 HEADROOM = 24.0
-DECAYED = 1024
+DECAYED = 768
 TURNED = 384
-EARLY = 768
+EARLY = 928
 
 
 def tile_attend_heavyhitter_kernel(tc, query, keys_words, keys_scales, mass, dec, offs, out):
@@ -68,10 +68,9 @@ def tile_attend_heavyhitter_kernel(tc, query, keys_words, keys_scales, mass, dec
         window_s = sb.tile([P, T], F32, name="window_s", tag="queries_then_window", align_bytes=64)
         nc.gpsimd.memset(window_s[:], 0.0)
 
-        old = shared.tile([P, T], F32, name="old", offset=I, align_bytes=64)
-        decay_tile = sb.tile([P, 1], F32, name="decay_tile")
-        decay = decay_tile[:]
-        nc.gpsimd.dma_start(out=decay, in_=dec)
+        old = shared.tile([P, T + 8], F32, name="old", offset=I, align_bytes=64)
+        decay = old[:, T : T + 1]
+        nc.sync.dma_start(out=decay, in_=dec)
         for lo, hi in ((0, DECAYED), (DECAYED, T)):
             nc.sync.dma_start(out=old[:, lo:hi], in_=mass[:, lo:hi])
         identity = sb.tile([P, P], F32, name="identity", tag="scales_then_identity", align_bytes=64)
@@ -171,30 +170,27 @@ def tile_attend_heavyhitter_kernel(tc, query, keys_words, keys_scales, mass, dec
         for b in blocks:
             turn(summed[b][:], carried[:, b * P : (b + 1) * P], False, False)
             turn(summed[b][:], window_s[:, columns[b]], False, True)
-        nc.scalar.activation(placed[:, 1024:1344], window_s[:, 1024:1344], ACT.Copy, scale=gain[:])
+        nc.scalar.activation(placed[:, 768:1152], window_s[:, 768:1152], ACT.Copy, scale=gain[:])
         for b in blocks:
             nc.scalar.copy(staged[b][:], summed[b][:])
             turn(back[b][:], staged[b][:], True, True)
-        nc.scalar.activation(placed[:, 1344:1664], window_s[:, 1344:1664], ACT.Copy, scale=gain[:])
+        nc.scalar.activation(placed[:, 1152:1664], window_s[:, 1152:1664], ACT.Copy, scale=gain[:])
         for b in blocks:
             nc.scalar.activation(res[:, columns[b]], back[b][:], ACT.Copy, scale=gain[:])
 
+        first_sum(DECAYED, EARLY)
         first_sum(0, 384)
-        first_sum(384, EARLY)
-        second_sum(0, 128)
-        store(0, 128)
-        second_sum(128, 384)
-        store(128, 384)
-        second_sum(384, 640)
-        store(384, 640)
-        first_sum(EARLY, 1024)
-        second_sum(640, EARLY)
-        second_sum(EARLY, 1024)
-        store(640, 1024)
-        first_sum(1024, 1344)
-        first_sum(1344, 1664)
+        first_sum(384, DECAYED)
+        for lo, hi in ((0, 128), (128, 384), (384, DECAYED)):
+            second_sum(lo, hi)
+            store(lo, hi)
+        first_sum(EARLY, 1152)
+        second_sum(DECAYED, EARLY)
+        second_sum(EARLY, 1152)
+        store(DECAYED, 1152)
         store(first_turned, T)
-        second_sum(1024, 1344)
-        store(1024, 1344)
-        second_sum(1344, 1664)
-        store(1344, 1664)
+        first_sum(1152, 1408)
+        first_sum(1408, 1664)
+        second_sum(1152, 1408)
+        second_sum(1408, 1664)
+        store(1152, 1664)

from contextlib import ExitStack

import concourse.mybir as mybir
from concourse.masks import make_identity

D, T, I, Q = 512, 2048, 512, 128
FLOPS = 2 * D * I * Q

F32 = mybir.dt.float32
BF16 = mybir.dt.bfloat16
I32 = mybir.dt.int32
U32 = mybir.dt.uint32
U16 = mybir.dt.uint16
U8 = mybir.dt.uint8
FP8X4 = mybir.dt.float8_e4m3fn_x4
FP4X4 = mybir.dt.float4_e2m1fn_x4
ALU = mybir.AluOpType
ACT = mybir.ActivationFunctionType

P = 128
PACK = 4
HALF = I // 2
HEADROOM = 24.0
DECAYED = 768
TURNED = 384
EARLY = 928


def tile_attend_heavyhitter_kernel(tc, query, keys_words, keys_scales, mass, dec, offs, out):
    nc = tc.nc
    with ExitStack() as ctx:
        sb = ctx.enter_context(tc.tile_pool(name="sb", bufs=1))
        shared = ctx.enter_context(tc.tile_pool(name="shared", bufs=1))
        ps = ctx.enter_context(tc.psum_pool(name="ps", bufs=1))

        offsets = sb.tile([P, I // 16], U16, name="offsets")
        pool_words = sb.tile([P, T], U16, name="pool_words", align_bytes=64)
        pool_scales = sb.tile([P, T], U8, name="pool_scales", tag="scales_then_identity", align_bytes=64)
        q_raw = shared.tile([P, PACK, Q], F32, name="q_raw", offset=0, align_bytes=64)
        window_v = sb.tile([P, T], F32, name="window_v")

        nc.vector.memset(pool_scales[:].bitcast(I32), 0)
        nc.sync.dma_start(out=q_raw[:], in_=query.rearrange("(p j) h -> p j h", j=PACK))
        nc.sync.dma_start(offsets[:], offs)
        for r in range(4):
            nc.sync.dma_start(out=pool_scales[r:P:32, :].bitcast(I32), in_=keys_scales[0, r:16:4, :].bitcast(I32))
        nc.sync.dma_start(out=pool_words[:].bitcast(I32), in_=keys_words[0].bitcast(I32))
        nc.vector.memset(window_v[:], 0.0)
        minus_one = sb.tile([P, 1], F32, name="minus_one")
        nc.vector.memset(minus_one[:], -1.0)

        q_grouped = sb.tile([P, Q, PACK], BF16, name="q_grouped", tag="queries_then_window", align_bytes=64)
        nc.vector.tensor_scalar(
            out=q_grouped[:].rearrange("p (c i) t -> p c t i", i=4),
            in0=q_raw[:].rearrange("p t (c i) -> p c t i", i=4),
            scalar1=-1.0,
            scalar2=None,
            op0=ALU.mult,
        )
        q_codes = sb.tile([P, Q], U32, name="q_codes", align_bytes=64)
        q_scales = sb.tile([P, Q], U8, name="q_scales", align_bytes=64)
        nc.vector.quantize_mx(
            out=q_codes[:].bitcast(FP8X4), scales=q_scales[:], in_=q_grouped[:].rearrange("p h t -> p (h t)")
        )
        k_scales = shared.tile([P, I], U8, name="k_scales", offset=0, align_bytes=64)
        nc.vector.tensor_copy(k_scales[:], pool_scales[:].indirect(offsets[:]))

        window_s = sb.tile([P, T], F32, name="window_s", tag="queries_then_window", align_bytes=64)
        nc.gpsimd.memset(window_s[:], 0.0)

        old = shared.tile([P, T + 8], F32, name="old", offset=I, align_bytes=64)
        decay = old[:, T : T + 1]
        nc.sync.dma_start(out=decay, in_=dec)
        for lo, hi in ((0, DECAYED), (DECAYED, T)):
            nc.sync.dma_start(out=old[:, lo:hi], in_=mass[:, lo:hi])
        identity = sb.tile([P, P], F32, name="identity", tag="scales_then_identity", align_bytes=64)
        make_identity(nc, identity[:])
        decay_share = sb.tile([P, 1], F32, name="decay_share")
        nc.scalar.activation(decay_share[:], decay, ACT.Copy, scale=1.0 / I)
        decayed = sb.tile([P, DECAYED], F32, name="decayed")
        nc.gpsimd.tensor_scalar(
            out=decayed[:], in0=old[:, :DECAYED], scalar1=decay, scalar2=0.0, op0=ALU.mult, op1=ALU.add
        )

        banks = []
        for h in range(2):
            k_words = sb.tile([P, HALF], U16, name="k_words%d" % h, align_bytes=64)
            nc.vector.tensor_copy(k_words[:], pool_words[:].indirect(offsets[:, h * HALF // 16 : (h + 1) * HALF // 16]))
            bank = ps.tile([P, HALF], F32, name="bank%d" % h)
            nc.tensor.matmul_mx(
                out=bank[:],
                lhsT=q_codes[:].bitcast(FP8X4),
                lhsT_scale=q_scales[:],
                rhs=k_words[:].bitcast(FP4X4),
                rhs_scale=k_scales[:, h * HALF : (h + 1) * HALF],
                start=True,
                stop=True,
            )
            banks.append(bank)

        spare = sb.tile([P, HALF], F32, name="spare")
        terms = sb.tile([P, I], F32, name="terms")
        sums = sb.tile([P, 2], F32, name="sums")
        shifts = [sb.tile([P, 1], F32, name="shift%d" % n) for n in range(2)]
        nc.vector.tensor_reduce(out=shifts[0][:], in_=banks[0][:], axis=mybir.AxisListType.X, op=ALU.min)
        nc.vector.tensor_scalar(
            out=spare[:], in0=banks[1][:], scalar1=HEADROOM, scalar2=shifts[0][:],
            op0=ALU.add, op1=ALU.min, accum_out=shifts[1][:],
        )
        for h in range(2):
            nc.scalar.activation(
                terms[:, h * HALF : (h + 1) * HALF], banks[h][:], ACT.Exp,
                bias=shifts[h][:], scale=-1.0, accum_out=sums[:, h : h + 1],
            )
        nc.vector.tensor_copy(window_v[:].indirect(offsets[:, : HALF // 16]), terms[:, :HALF])
        nc.scalar.activation(window_s[:].indirect(offsets[:, HALF // 16 :]), terms[:, HALF:], ACT.Copy)

        mean = sb.tile([P, 1], F32, name="mean")
        carry = sb.tile([P, 1], F32, name="carry")
        gain = sb.tile([P, 1], F32, name="gain")
        nc.gpsimd.tensor_scalar(
            out=mean[:], in0=sums[:, 0:1], scalar1=sums[:, 1:2], scalar2=1.0 / I, op0=ALU.add, op1=ALU.mult
        )
        nc.gpsimd.tensor_scalar(
            out=carry[:], in0=sums[:, 0:1], scalar1=sums[:, 1:2], scalar2=decay_share[:], op0=ALU.add, op1=ALU.mult
        )
        nc.gpsimd.tensor_tensor(out=gain[:], in0=mean[:], in1=minus_one[:], op=ALU.pow)

        first_turned = T - TURNED
        carried = sb.tile([P, TURNED], F32, name="carried")
        nc.vector.tensor_scalar(
            out=carried[:], in0=old[:, first_turned:T], scalar1=carry[:], scalar2=None, op0=ALU.mult
        )

        partial = sb.tile([P, first_turned], F32, name="partial")
        placed = sb.tile([P, first_turned], F32, name="placed")
        res = sb.tile([P, T], F32, name="res")

        def first_sum(lo, hi):
            if hi <= DECAYED:
                scaled, factor, added = window_v[:, lo:hi], gain[:], decayed[:, lo:hi]
            else:
                scaled, factor, added = old[:, lo:hi], carry[:], window_v[:, lo:hi]
            nc.vector.scalar_tensor_tensor(
                out=partial[:, lo:hi], in0=scaled, scalar=factor, in1=added, op0=ALU.mult, op1=ALU.add
            )

        def second_sum(lo, hi):
            if hi <= DECAYED:
                scaled, added = window_s[:, lo:hi], partial[:, lo:hi]
            else:
                scaled, added = partial[:, lo:hi], placed[:, lo:hi]
            nc.vector.scalar_tensor_tensor(
                out=res[:, lo:hi], in0=scaled, scalar=gain[:], in1=added, op0=ALU.mult, op1=ALU.add
            )

        def store(lo, hi):
            nc.sync.dma_start(out=out[:, lo:hi], in_=res[:, lo:hi])

        def turn(bank, source, start, stop):
            nc.tensor.matmul(bank, lhsT=source, rhs=identity[:], is_transpose=True, start=start, stop=stop)

        blocks = range(TURNED // P)
        summed = [ps.tile([P, P], F32, name="summed%d" % b) for b in blocks]
        back = [ps.tile([P, P], F32, name="back%d" % b) for b in blocks]
        staged = [sb.tile([P, P], F32, name="staged%d" % b) for b in blocks]
        columns = [slice(first_turned + b * P, first_turned + (b + 1) * P) for b in blocks]
        for b in blocks:
            turn(summed[b][:], window_v[:, columns[b]], True, False)
        for b in blocks:
            turn(summed[b][:], carried[:, b * P : (b + 1) * P], False, False)
            turn(summed[b][:], window_s[:, columns[b]], False, True)
        nc.scalar.activation(placed[:, 768:1152], window_s[:, 768:1152], ACT.Copy, scale=gain[:])
        for b in blocks:
            nc.scalar.copy(staged[b][:], summed[b][:])
            turn(back[b][:], staged[b][:], True, True)
        nc.scalar.activation(placed[:, 1152:1664], window_s[:, 1152:1664], ACT.Copy, scale=gain[:])
        for b in blocks:
            nc.scalar.activation(res[:, columns[b]], back[b][:], ACT.Copy, scale=gain[:])

        first_sum(DECAYED, EARLY)
        first_sum(0, 384)
        first_sum(384, DECAYED)
        for lo, hi in ((0, 128), (128, 384), (384, DECAYED)):
            second_sum(lo, hi)
            store(lo, hi)
        first_sum(EARLY, 1152)
        second_sum(DECAYED, EARLY)
        second_sum(EARLY, 1152)
        store(DECAYED, 1152)
        store(first_turned, T)
        first_sum(1152, 1408)
        first_sum(1408, 1664)
        second_sum(1152, 1408)
        second_sum(1408, 1664)
        store(1152, 1664)
